import numpy as np
import ml_dtypes


def mxq(x, axis, fmt="e4m3"):
    dtype, down = {"e4m3": (ml_dtypes.float8_e4m3fn, 7), "e5m2": (ml_dtypes.float8_e5m2, 14)}[fmt]
    v = np.moveaxis(np.asarray(x, np.float32).astype(ml_dtypes.bfloat16).astype(np.float64), axis, -1)
    blocks = v.reshape(v.shape[:-1] + (-1, 32))
    amax = np.abs(blocks).max(-1, keepdims=True)
    byte = np.maximum(np.where(amax > 0, np.frexp(amax)[1] - 1 + 127, 0) - down, 1)
    scale = np.exp2(byte - 127.0)
    codes = (blocks / scale).astype(np.float32).astype(dtype).astype(np.float64)
    return np.moveaxis((codes * scale).reshape(v.shape), -1, axis)


WIDE = False


def mx_kscale(k):
    if not WIDE:
        return np.ones(k)
    levels = np.array([10, -10, 5, -5, 0])
    if k % 512:
        return np.exp2(np.random.permutation(np.resize(levels, k // 32))).repeat(32)
    a = np.empty((k // 512, 16))
    for p in range(k // 512):
        a[p, :8] = np.random.permutation(np.resize(levels, 8))
        for g in range(8):
            far = levels[np.abs(levels - a[p, g]) >= 10]
            a[p, g + 8] = far[np.random.randint(len(far))]
    return np.exp2(a.ravel()).repeat(32)


def f64(x):
    return np.asarray(x).astype(np.float64)


def striped(idx):
    return np.tile(idx.reshape(-1, 16).T, (8, 1)).astype(np.uint16)


def unstriped(offs):
    return offs[:16].T.reshape(-1).astype(np.int64)


def relu(v):
    return np.maximum(v, 0.0)


K, T, D, S, V, N = 1024, 2048, 4, 512, 128, 512


def setup_inputs():
    n = np.random.standard_normal
    s = mx_kscale(K)[:, None]
    return {
        "xT": (n((K, T)) * s).astype(np.float32),
        "w": (n((D, K, N)) / np.sqrt(D * K) / s[None]).astype(np.float32),
        "b": (0.3 * n((N, 1))).astype(np.float32),
        "offs": striped(np.random.permutation(T)[:S]),
    }


def reference(xT, w, b, offs):
    idx = unstriped(offs)
    xq = mxq(f64(xT)[:, idx], 0, "e4m3")
    wq = mxq(f64(w), 1, "e4m3")
    y = sum(wq[d].T @ xq[:, d * V:(d + 1) * V] for d in range(D))
    y = relu(y + f64(b))
    return y

@@ -1,0 +1,158 @@
+from contextlib import ExitStack
+
+import concourse.mybir as mybir
+from concourse.masks import make_identity
+
+K, T, D, S, V, N = 1024, 2048, 4, 512, 128, 512
+FLOPS = 2 * K * N * S
+
+F32 = mybir.dt.float32
+BF16 = mybir.dt.bfloat16
+U32 = mybir.dt.uint32
+U16 = mybir.dt.uint16
+U8 = mybir.dt.uint8
+FP8X4 = mybir.dt.float8_e4m3fn_x4
+RELU = mybir.ActivationFunctionType.Relu
+ADD, MAX = mybir.AluOpType.add, mybir.AluOpType.max
+
+P = 128
+PACK = 4
+K_PASS = P * PACK
+PASSES = K // K_PASS
+M_TILES = N // P
+
+
+def tile_picked_merge_lin_relu_sub_e_kernel(tc, xT, w, b, offs, out):
+    nc = tc.nc
+    x_rows = xT.rearrange("(a p j) t -> a p j t", a=PASSES, j=PACK)
+    w_rows = w.rearrange("d (a p j) m -> d a p j m", a=PASSES, j=PACK)
+
+    with ExitStack() as ctx:
+        held = ctx.enter_context(tc.tile_pool(name="held", bufs=1))
+        ring = ctx.enter_context(tc.tile_pool(name="ring", bufs=4))
+        psum = ctx.enter_context(tc.psum_pool(name="psum", bufs=1))
+
+        offsets = held.tile([P, S // 16], U16, name="offsets")
+        bias_rows = held.tile([P, P], F32, name="bias_rows")
+        bias = held.tile([P, M_TILES], F32, name="bias")
+        ident = held.tile([P, P], F32, name="ident")
+        planes, raws, groupeds, codes, scales = {}, {}, {}, {}, {}
+        picked = [held.tile([P, PACK, S], F32, name=f"picked{a}") for a in range(PASSES)]
+        x_codes = [held.tile([P, S], U32, align_bytes=64, name=f"x_codes{a}") for a in range(PASSES)]
+        x_scales = [held.tile([P, S], U8, align_bytes=64, name=f"x_scales{a}") for a in range(PASSES)]
+        acc = [psum.tile([P, V], F32, name=f"acc{t}") for t in range(M_TILES)]
+        results = [held.tile([P, V], F32, name=f"result{t}") for t in range(M_TILES)]
+
+        def load_x(a, j0):
+            planes[a, j0] = held.tile([P, 2, T], F32, name=f"planes{a}{j0}")
+            nc.sync.dma_start(planes[a, j0][:], x_rows[a, :, j0 : j0 + 2, :])
+
+        def load_w(d, a, c0, c1):
+            raws[d, a, c0] = held.tile([P, PACK, c1 - c0], F32, name=f"raw{d}{a}{c0}")
+            nc.sync.dma_start(raws[d, a, c0][:], w_rows[d, a, :, :, c0:c1])
+
+        def interleave(dst, src, c0, c1, engine_copy):
+            engine_copy(
+                dst[:, c0:c1, :].rearrange("p (c i) j -> p c j i", i=4),
+                src[:, :, c0:c1].rearrange("p j (c i) -> p c j i", i=4),
+            )
+
+        def gather(a, j0):
+            for u in range(2):
+                nc.vector.tensor_copy(picked[a][:, j0 + u, :], planes[a, j0][:, u, :].indirect(offsets[:]))
+
+        def spread_x(a, c0, c1):
+            if c0 == 0:
+                groupeds[a] = ring.tile([P, S, PACK], BF16, align_bytes=64, name="x_grouped")
+            interleave(groupeds[a], picked[a], c0, c1, nc.scalar.copy)
+
+        def quantise_x(a):
+            nc.vector.quantize_mx(
+                out=x_codes[a][:].bitcast(FP8X4),
+                scales=x_scales[a][:],
+                in_=groupeds[a][:].rearrange("p c j -> p (c j)"),
+            )
+
+        def spread_w(d, a, c0, c1, v_cols):
+            width = c1 - c0
+            grouped = ring.tile([P, width, PACK], BF16, align_bytes=64, name=f"w_grouped{width}")
+            groupeds[d, a, c0] = grouped
+            interleave(grouped, raws[d, a, c0], 0, v_cols, nc.vector.tensor_copy)
+            interleave(grouped, raws[d, a, c0], v_cols, width, nc.scalar.copy)
+
+        def quantise_w(d, a, c0, c1):
+            codes[d, a, c0] = held.tile([P, c1 - c0], U32, align_bytes=64, name=f"w_codes{d}{a}{c0}")
+            scales[d, a, c0] = held.tile([P, c1 - c0], U8, align_bytes=64, name=f"w_scales{d}{a}{c0}")
+            nc.vector.quantize_mx(
+                out=codes[d, a, c0][:].bitcast(FP8X4),
+                scales=scales[d, a, c0][:],
+                in_=groupeds[d, a, c0][:].rearrange("p c j -> p (c j)"),
+            )
+
+        def multiply(d, a, c0, c1, first=False, last=False):
+            tokens = slice(d * V, (d + 1) * V)
+            for m0 in range(c0, c1, P):
+                cols = slice(m0 - c0, m0 - c0 + P)
+                nc.tensor.matmul_mx(
+                    out=acc[m0 // P][:],
+                    lhsT=codes[d, a, c0][:, cols].bitcast(FP8X4),
+                    lhsT_scale=scales[d, a, c0][:, cols],
+                    rhs=x_codes[a][:, tokens].bitcast(FP8X4),
+                    rhs_scale=x_scales[a][:, tokens],
+                    start=first,
+                    stop=last,
+                )
+
+        def finish(t, on_vector=False):
+            if on_vector:
+                nc.vector.tensor_scalar(results[t][:], acc[t][:], bias[:, t : t + 1], 0.0, op0=ADD, op1=MAX)
+            else:
+                nc.scalar.activation(results[t][:], acc[t][:], RELU, bias=bias[:, t : t + 1])
+            nc.sync.dma_start(out[t * P : (t + 1) * P, :], results[t][:])
+
+        nc.gpsimd.memset(bias_rows[:], 0.0)
+        make_identity(nc, ident[:])
+        turned = psum.tile([P, P], F32, name="turned")
+
+        def turn_bias():
+            nc.tensor.transpose(turned[:], bias_rows[:], ident[:])
+            nc.vector.tensor_copy(bias[:], turned[:, 0:M_TILES])
+
+        load_x(0, 0)
+        nc.sync.dma_start(offsets[:], offs)
+        load_x(0, 2)
+        nc.sync.dma_start(bias_rows[0:M_TILES, :], b.rearrange("(t p) o -> t (p o)", p=P))
+        load_x(1, 0)
+        load_x(1, 2)
+        chunks = [(d, a, 0, N) for a in range(PASSES) for d in range(D)][:-1]
+        chunks += [(3, 1, 0, 256), (3, 1, 256, 384), (3, 1, 384, 512)]
+        for chunk in chunks:
+            load_w(*chunk)
+
+        gather(0, 0)
+        gather(0, 2)
+        spread_x(0, 0, S)
+        gather(1, 0)
+        quantise_x(0)
+        turn_bias()
+        gather(1, 2)
+        spread_w(*chunks[0], 224)
+        spread_x(1, 0, 256)
+        spread_w(*chunks[1], 224)
+        quantise_w(*chunks[0])
+        multiply(*chunks[0], first=True)
+        spread_x(1, 256, S)
+        spread_w(*chunks[2], 224)
+        quantise_w(*chunks[1])
+        multiply(*chunks[1])
+        quantise_x(1)
+        for before, now in zip(chunks[2:], chunks[3:]):
+            spread_w(*now, 224 if now[3] - now[2] == N else (now[3] - now[2]) // 2)
+            quantise_w(*before)
+            multiply(*before, last=before[:2] == (3, 1))
+        quantise_w(*chunks[-1])
+        multiply(*chunks[-1], last=True)
+        finish(0)
+        finish(1)
+        finish(2)
+        finish(3, on_vector=True)

@@ -25,134 +25,158 @@ M_TILES = N // P
 def tile_picked_merge_lin_relu_sub_e_kernel(tc, xT, w, b, offs, out):
     nc = tc.nc
     x_rows = xT.rearrange("(a p j) t -> a p j t", a=PASSES, j=PACK)
-    w_rows = w.rearrange("d (a p j) m -> d a p j m", a=PASSES, j=PACK)
+    w_rows = w.rearrange("d (a p j) m -> p (d a) j m", a=PASSES, j=PACK)
 
     with ExitStack() as ctx:
         held = ctx.enter_context(tc.tile_pool(name="held", bufs=1))
-        ring = ctx.enter_context(tc.tile_pool(name="ring", bufs=4))
         psum = ctx.enter_context(tc.psum_pool(name="psum", bufs=1))
 
         offsets = held.tile([P, S // 16], U16, name="offsets")
         bias_rows = held.tile([P, P], F32, name="bias_rows")
         bias = held.tile([P, M_TILES], F32, name="bias")
         ident = held.tile([P, P], F32, name="ident")
-        planes, raws, groupeds, codes, scales = {}, {}, {}, {}, {}
+        raws, groupeds, codes, scales = {}, {}, {}, {}
+        planes = [held.tile([P, PACK, T], F32, name=f"planes{a}") for a in range(PASSES)]
         picked = [held.tile([P, PACK, S], F32, name=f"picked{a}") for a in range(PASSES)]
+        x_grouped = {0: held.tile([P, S, PACK], BF16, align_bytes=64, name="x_grouped0")}
         x_codes = [held.tile([P, S], U32, align_bytes=64, name=f"x_codes{a}") for a in range(PASSES)]
         x_scales = [held.tile([P, S], U8, align_bytes=64, name=f"x_scales{a}") for a in range(PASSES)]
         acc = [psum.tile([P, V], F32, name=f"acc{t}") for t in range(M_TILES)]
-        results = [held.tile([P, V], F32, name=f"result{t}") for t in range(M_TILES)]
+        result = held.tile([P, M_TILES, V], F32, name="result")
+        out_tiles = out.rearrange("(t p) v -> p t v", p=P)
 
-        def load_x(a, j0):
-            planes[a, j0] = held.tile([P, 2, T], F32, name=f"planes{a}{j0}")
-            nc.sync.dma_start(planes[a, j0][:], x_rows[a, :, j0 : j0 + 2, :])
+        def load_chunks(first, count):
+            raw = held.tile([P, count, PACK, N], F32, align_bytes=64, name=f"raw{first}", tag=f"raw{first}")
+            nc.sync.dma_start(
+                raw[:].rearrange("p c j m -> p c (j m)"),
+                w_rows[:, first : first + count, :, :].rearrange("p c j m -> p c (j m)"),
+            )
+            for c in range(count):
+                raws[first + c, 0] = raw[:, c, :, :]
 
-        def load_w(d, a, c0, c1):
-            raws[d, a, c0] = held.tile([P, PACK, c1 - c0], F32, name=f"raw{d}{a}{c0}")
-            nc.sync.dma_start(raws[d, a, c0][:], w_rows[d, a, :, :, c0:c1])
+        def load_columns(chunk, c0, c1):
+            raw = held.tile([P, PACK, c1 - c0], F32, name=f"raw{chunk}_{c0}")
+            nc.sync.dma_start(raw[:], w_rows[:, chunk, :, c0:c1])
+            raws[chunk, c0] = raw[:]
 
-        def interleave(dst, src, c0, c1, engine_copy):
+        def interleave(dst, src, engine_copy):
             engine_copy(
-                dst[:, c0:c1, :].rearrange("p (c i) j -> p c j i", i=4),
-                src[:, :, c0:c1].rearrange("p j (c i) -> p c j i", i=4),
+                dst.rearrange("p (c i) j -> p c j i", i=4),
+                src.rearrange("p j (c i) -> p c j i", i=4),
             )
 
-        def gather(a, j0):
-            for u in range(2):
-                nc.vector.tensor_copy(picked[a][:, j0 + u, :], planes[a, j0][:, u, :].indirect(offsets[:]))
-
-        def spread_x(a, c0, c1):
-            if c0 == 0:
-                groupeds[a] = ring.tile([P, S, PACK], BF16, align_bytes=64, name="x_grouped")
-            interleave(groupeds[a], picked[a], c0, c1, nc.scalar.copy)
+        def gather(a):
+            for j in range(PACK):
+                nc.vector.tensor_copy(picked[a][:, j, :], planes[a][:, j, :].indirect(offsets[:]))
 
         def quantise_x(a):
             nc.vector.quantize_mx(
                 out=x_codes[a][:].bitcast(FP8X4),
                 scales=x_scales[a][:],
-                in_=groupeds[a][:].rearrange("p c j -> p (c j)"),
+                in_=x_grouped[a][:].rearrange("p c j -> p (c j)"),
             )
 
-        def spread_w(d, a, c0, c1, v_cols):
-            width = c1 - c0
-            grouped = ring.tile([P, width, PACK], BF16, align_bytes=64, name=f"w_grouped{width}")
-            groupeds[d, a, c0] = grouped
-            interleave(grouped, raws[d, a, c0], 0, v_cols, nc.vector.tensor_copy)
-            interleave(grouped, raws[d, a, c0], v_cols, width, nc.scalar.copy)
+        def new_part(chunk, c0, c1):
+            groupeds[chunk, c0] = held.tile([P, c1 - c0, PACK], BF16, align_bytes=64, name=f"w_grouped{chunk}_{c0}")
 
-        def quantise_w(d, a, c0, c1):
-            codes[d, a, c0] = held.tile([P, c1 - c0], U32, align_bytes=64, name=f"w_codes{d}{a}{c0}")
-            scales[d, a, c0] = held.tile([P, c1 - c0], U8, align_bytes=64, name=f"w_scales{d}{a}{c0}")
+        def spread(chunk, load0, part0, c0, c1, engine_copy):
+            interleave(
+                groupeds[chunk, part0][:, c0 - part0 : c1 - part0, :],
+                raws[chunk, load0][:, :, c0 - load0 : c1 - load0],
+                engine_copy,
+            )
+
+        def finish_part(chunk, c0, c1):
+            w_codes = held.tile([P, c1 - c0], U32, align_bytes=64, name=f"w_codes{chunk}_{c0}")
+            w_scales = held.tile([P, c1 - c0], U8, align_bytes=64, name=f"w_scales{chunk}_{c0}")
             nc.vector.quantize_mx(
-                out=codes[d, a, c0][:].bitcast(FP8X4),
-                scales=scales[d, a, c0][:],
-                in_=groupeds[d, a, c0][:].rearrange("p c j -> p (c j)"),
+                out=w_codes[:].bitcast(FP8X4),
+                scales=w_scales[:],
+                in_=groupeds[chunk, c0][:].rearrange("p c j -> p (c j)"),
             )
-
-        def multiply(d, a, c0, c1, first=False, last=False):
+            d, a = divmod(chunk, PASSES)
             tokens = slice(d * V, (d + 1) * V)
             for m0 in range(c0, c1, P):
                 cols = slice(m0 - c0, m0 - c0 + P)
                 nc.tensor.matmul_mx(
                     out=acc[m0 // P][:],
-                    lhsT=codes[d, a, c0][:, cols].bitcast(FP8X4),
-                    lhsT_scale=scales[d, a, c0][:, cols],
+                    lhsT=w_codes[:, cols].bitcast(FP8X4),
+                    lhsT_scale=w_scales[:, cols],
                     rhs=x_codes[a][:, tokens].bitcast(FP8X4),
                     rhs_scale=x_scales[a][:, tokens],
-                    start=first,
-                    stop=last,
+                    start=chunk == 0,
+                    stop=chunk == D * PASSES - 1,
                 )
 
-        def finish(t, on_vector=False):
+        def emit(t, on_vector=False):
             if on_vector:
-                nc.vector.tensor_scalar(results[t][:], acc[t][:], bias[:, t : t + 1], 0.0, op0=ADD, op1=MAX)
+                nc.vector.tensor_scalar(result[:, t, :], acc[t][:], bias[:, t : t + 1], 0.0, op0=ADD, op1=MAX)
             else:
-                nc.scalar.activation(results[t][:], acc[t][:], RELU, bias=bias[:, t : t + 1])
-            nc.sync.dma_start(out[t * P : (t + 1) * P, :], results[t][:])
+                nc.scalar.activation(result[:, t, :], acc[t][:], RELU, bias=bias[:, t : t + 1])
+
+        def store(t0, t1, queue):
+            queue.dma_start(out_tiles[:, t0:t1, :], result[:, t0:t1, :])
 
         nc.gpsimd.memset(bias_rows[:], 0.0)
         make_identity(nc, ident[:])
         turned = psum.tile([P, P], F32, name="turned")
 
-        def turn_bias():
-            nc.tensor.transpose(turned[:], bias_rows[:], ident[:])
-            nc.vector.tensor_copy(bias[:], turned[:, 0:M_TILES])
-
-        load_x(0, 0)
+        nc.sync.dma_start(planes[0][:], x_rows[0])
         nc.sync.dma_start(offsets[:], offs)
-        load_x(0, 2)
         nc.sync.dma_start(bias_rows[0:M_TILES, :], b.rearrange("(t p) o -> t (p o)", p=P))
-        load_x(1, 0)
-        load_x(1, 2)
-        chunks = [(d, a, 0, N) for a in range(PASSES) for d in range(D)][:-1]
-        chunks += [(3, 1, 0, 256), (3, 1, 256, 384), (3, 1, 384, 512)]
-        for chunk in chunks:
-            load_w(*chunk)
+        nc.sync.dma_start(planes[1][:], x_rows[1])
+        load_chunks(0, 1)
+        load_chunks(1, 2)
+        load_chunks(3, 1)
+        load_chunks(4, 1)
+        load_chunks(5, 1)
+        load_chunks(6, 1)
+        last = D * PASSES - 1
+        load_columns(last, 0, 256)
+        load_columns(last, 256, 384)
+        load_columns(last, 384, 512)
 
-        gather(0, 0)
-        gather(0, 2)
-        spread_x(0, 0, S)
-        gather(1, 0)
+        gather(0)
+        interleave(x_grouped[0][:], picked[0][:], nc.scalar.copy)
+        nc.tensor.transpose(turned[:], bias_rows[:], ident[:])
+        nc.vector.tensor_copy(bias[:], turned[:, 0:M_TILES])
         quantise_x(0)
-        turn_bias()
-        gather(1, 2)
-        spread_w(*chunks[0], 224)
-        spread_x(1, 0, 256)
-        spread_w(*chunks[1], 224)
-        quantise_w(*chunks[0])
-        multiply(*chunks[0], first=True)
-        spread_x(1, 256, S)
-        spread_w(*chunks[2], 224)
-        quantise_w(*chunks[1])
-        multiply(*chunks[1])
-        quantise_x(1)
-        for before, now in zip(chunks[2:], chunks[3:]):
-            spread_w(*now, 224 if now[3] - now[2] == N else (now[3] - now[2]) // 2)
-            quantise_w(*before)
-            multiply(*before, last=before[:2] == (3, 1))
-        quantise_w(*chunks[-1])
-        multiply(*chunks[-1], last=True)
-        finish(0)
-        finish(1)
-        finish(2)
-        finish(3, on_vector=True)
+        gather(1)
+        share = 224
+        new_part(0, 0, N)
+        spread(0, 0, 0, 0, N, nc.scalar.copy)
+        x_grouped[1] = held.tile([P, S, PACK], BF16, align_bytes=64, name="x_grouped1", tag="raw0")
+        interleave(x_grouped[1][:, :share, :], picked[1][:, :, :share], nc.vector.tensor_copy)
+        interleave(x_grouped[1][:, share:, :], picked[1][:, :, share:], nc.scalar.copy)
+        finish_part(0, 0, N)
+        for chunk in range(1, last - 1):
+            new_part(chunk, 0, N)
+            spread(chunk, 0, 0, 0, share, nc.vector.tensor_copy)
+            spread(chunk, 0, 0, share, N, nc.scalar.copy)
+            if chunk == 1:
+                quantise_x(1)
+            else:
+                finish_part(chunk - 1, 0, N)
+        finish_part(last - 2, 0, N)
+        new_part(last - 1, 0, N)
+        spread(last - 1, 0, 0, 0, 256, nc.vector.tensor_copy)
+        spread(last - 1, 0, 0, 256, N, nc.scalar.copy)
+        new_part(last, 0, 256)
+        new_part(last, 256, 384)
+        new_part(last, 384, 512)
+        spread(last, 0, 0, 0, 128, nc.vector.tensor_copy)
+        spread(last, 0, 0, 128, 256, nc.scalar.copy)
+        finish_part(last - 1, 0, N)
+        spread(last, 256, 256, 256, 384, nc.scalar.copy)
+        finish_part(last, 0, 256)
+        spread(last, 384, 384, 384, 448, nc.vector.tensor_copy)
+        spread(last, 384, 384, 448, 512, nc.scalar.copy)
+        finish_part(last, 256, 384)
+        finish_part(last, 384, 512)
+        emit(0)
+        emit(1)
+        store(0, 2, nc.sync)
+        emit(2)
+        store(2, 3, nc.sync)
+        emit(3, on_vector=True)
+        store(3, 4, nc.scalar)

@@ -127,8 +127,7 @@ def tile_picked_merge_lin_relu_sub_e_kernel(tc, xT, w, b, offs, out):
         nc.sync.dma_start(planes[1][:], x_rows[1])
         load_chunks(0, 1)
         load_chunks(1, 2)
-        load_chunks(3, 1)
-        load_chunks(4, 1)
+        load_chunks(3, 2)
         load_chunks(5, 1)
         load_chunks(6, 1)
         last = D * PASSES - 1
@@ -175,8 +174,8 @@ def tile_picked_merge_lin_relu_sub_e_kernel(tc, xT, w, b, offs, out):
         finish_part(last, 384, 512)
         emit(0)
         emit(1)
-        store(0, 2, nc.sync)
+        store(0, 2, nc.scalar)
         emit(2)
-        store(2, 3, nc.sync)
+        store(2, 3, nc.scalar)
         emit(3, on_vector=True)
-        store(3, 4, nc.scalar)
+        store(3, 4, nc.sync)

@@ -20,6 +20,7 @@ PACK = 4
 K_PASS = P * PACK
 PASSES = K // K_PASS
 M_TILES = N // P
+DMA_ALIGN = 512
 
 
 def tile_picked_merge_lin_relu_sub_e_kernel(tc, xT, w, b, offs, out):
@@ -36,17 +37,17 @@ def tile_picked_merge_lin_relu_sub_e_kernel(tc, xT, w, b, offs, out):
         bias = held.tile([P, M_TILES], F32, name="bias")
         ident = held.tile([P, P], F32, name="ident")
         raws, groupeds, codes, scales = {}, {}, {}, {}
-        planes = [held.tile([P, PACK, T], F32, name=f"planes{a}") for a in range(PASSES)]
+        planes = [held.tile([P, PACK, T], F32, align_bytes=DMA_ALIGN, name=f"planes{a}") for a in range(PASSES)]
         picked = [held.tile([P, PACK, S], F32, name=f"picked{a}") for a in range(PASSES)]
         x_grouped = {0: held.tile([P, S, PACK], BF16, align_bytes=64, name="x_grouped0")}
         x_codes = [held.tile([P, S], U32, align_bytes=64, name=f"x_codes{a}") for a in range(PASSES)]
         x_scales = [held.tile([P, S], U8, align_bytes=64, name=f"x_scales{a}") for a in range(PASSES)]
         acc = [psum.tile([P, V], F32, name=f"acc{t}") for t in range(M_TILES)]
-        result = held.tile([P, M_TILES, V], F32, name="result")
+        result = held.tile([P, M_TILES, V], F32, align_bytes=DMA_ALIGN, name="result")
         out_tiles = out.rearrange("(t p) v -> p t v", p=P)
 
         def load_chunks(first, count):
-            raw = held.tile([P, count, PACK, N], F32, align_bytes=64, name=f"raw{first}", tag=f"raw{first}")
+            raw = held.tile([P, count, PACK, N], F32, align_bytes=DMA_ALIGN, name=f"raw{first}", tag=f"raw{first}")
             nc.sync.dma_start(
                 raw[:].rearrange("p c j m -> p c (j m)"),
                 w_rows[:, first : first + count, :, :].rearrange("p c j m -> p c (j m)"),
@@ -55,7 +56,7 @@ def tile_picked_merge_lin_relu_sub_e_kernel(tc, xT, w, b, offs, out):
                 raws[first + c, 0] = raw[:, c, :, :]
 
         def load_columns(chunk, c0, c1):
-            raw = held.tile([P, PACK, c1 - c0], F32, name=f"raw{chunk}_{c0}")
+            raw = held.tile([P, PACK, c1 - c0], F32, align_bytes=DMA_ALIGN, name=f"raw{chunk}_{c0}")
             nc.sync.dma_start(raw[:], w_rows[:, chunk, :, c0:c1])
             raws[chunk, c0] = raw[:]
 
@@ -144,7 +145,7 @@ def tile_picked_merge_lin_relu_sub_e_kernel(tc, xT, w, b, offs, out):
         share = 224
         new_part(0, 0, N)
         spread(0, 0, 0, 0, N, nc.scalar.copy)
-        x_grouped[1] = held.tile([P, S, PACK], BF16, align_bytes=64, name="x_grouped1", tag="raw0")
+        x_grouped[1] = held.tile([P, S, PACK], BF16, align_bytes=DMA_ALIGN, name="x_grouped1", tag="raw0")
         interleave(x_grouped[1][:, :share, :], picked[1][:, :, :share], nc.vector.tensor_copy)
         interleave(x_grouped[1][:, share:, :], picked[1][:, :, share:], nc.scalar.copy)
         finish_part(0, 0, N)

@@ -20,7 +20,11 @@ PACK = 4
 K_PASS = P * PACK
 PASSES = K // K_PASS
 M_TILES = N // P
-DMA_ALIGN = 512
+DMA_ALIGN = 4096
+LINE_ALIGN = 256
+PLANES_BYTES = PACK * T * 4
+CHUNK_BYTES = PACK * N * 4
+W_AT = PASSES * PLANES_BYTES
 
 
 def tile_picked_merge_lin_relu_sub_e_kernel(tc, xT, w, b, offs, out):
@@ -29,25 +33,26 @@ def tile_picked_merge_lin_relu_sub_e_kernel(tc, xT, w, b, offs, out):
     w_rows = w.rearrange("d (a p j) m -> p (d a) j m", a=PASSES, j=PACK)
 
     with ExitStack() as ctx:
+        moved = ctx.enter_context(tc.tile_pool(name="moved", bufs=1))
         held = ctx.enter_context(tc.tile_pool(name="held", bufs=1))
         psum = ctx.enter_context(tc.psum_pool(name="psum", bufs=1))
 
-        offsets = held.tile([P, S // 16], U16, name="offsets")
-        bias_rows = held.tile([P, P], F32, name="bias_rows")
-        bias = held.tile([P, M_TILES], F32, name="bias")
-        ident = held.tile([P, P], F32, name="ident")
+        offsets = held.tile([P, S // 16], U16, align_bytes=LINE_ALIGN, name="offsets")
+        bias_rows = held.tile([P, P], F32, align_bytes=LINE_ALIGN, name="bias_rows")
+        bias = held.tile([P, M_TILES], F32, align_bytes=LINE_ALIGN, name="bias")
+        ident = held.tile([P, P], F32, align_bytes=LINE_ALIGN, name="ident")
         raws, groupeds, codes, scales = {}, {}, {}, {}
-        planes = [held.tile([P, PACK, T], F32, align_bytes=DMA_ALIGN, name=f"planes{a}") for a in range(PASSES)]
-        picked = [held.tile([P, PACK, S], F32, name=f"picked{a}") for a in range(PASSES)]
-        x_grouped = {0: held.tile([P, S, PACK], BF16, align_bytes=64, name="x_grouped0")}
-        x_codes = [held.tile([P, S], U32, align_bytes=64, name=f"x_codes{a}") for a in range(PASSES)]
-        x_scales = [held.tile([P, S], U8, align_bytes=64, name=f"x_scales{a}") for a in range(PASSES)]
+        planes = [moved.tile([P, PACK, T], F32, align_bytes=DMA_ALIGN, offset=a * PLANES_BYTES, name=f"planes{a}") for a in range(PASSES)]
+        picked = [held.tile([P, PACK, S], F32, align_bytes=LINE_ALIGN, name=f"picked{a}") for a in range(PASSES)]
+        x_grouped = {0: held.tile([P, S, PACK], BF16, align_bytes=LINE_ALIGN, name="x_grouped0")}
+        x_codes = [held.tile([P, S], U32, align_bytes=LINE_ALIGN, name=f"x_codes{a}") for a in range(PASSES)]
+        x_scales = [held.tile([P, S], U8, align_bytes=LINE_ALIGN, name=f"x_scales{a}") for a in range(PASSES)]
         acc = [psum.tile([P, V], F32, name=f"acc{t}") for t in range(M_TILES)]
-        result = held.tile([P, M_TILES, V], F32, align_bytes=DMA_ALIGN, name="result")
+        result = moved.tile([P, M_TILES, V], F32, align_bytes=DMA_ALIGN, offset=W_AT + D * PASSES * CHUNK_BYTES + DMA_ALIGN, name="result")
         out_tiles = out.rearrange("(t p) v -> p t v", p=P)
 
         def load_chunks(first, count):
-            raw = held.tile([P, count, PACK, N], F32, align_bytes=DMA_ALIGN, name=f"raw{first}", tag=f"raw{first}")
+            raw = moved.tile([P, count, PACK, N], F32, align_bytes=DMA_ALIGN, offset=W_AT + first * CHUNK_BYTES, name=f"raw{first}", tag=f"raw{first}")
             nc.sync.dma_start(
                 raw[:].rearrange("p c j m -> p c (j m)"),
                 w_rows[:, first : first + count, :, :].rearrange("p c j m -> p c (j m)"),
@@ -55,8 +60,8 @@ def tile_picked_merge_lin_relu_sub_e_kernel(tc, xT, w, b, offs, out):
             for c in range(count):
                 raws[first + c, 0] = raw[:, c, :, :]
 
-        def load_columns(chunk, c0, c1):
-            raw = held.tile([P, PACK, c1 - c0], F32, align_bytes=DMA_ALIGN, name=f"raw{chunk}_{c0}")
+        def load_columns(chunk, c0, c1, slot):
+            raw = moved.tile([P, PACK, c1 - c0], F32, align_bytes=DMA_ALIGN, offset=W_AT + chunk * CHUNK_BYTES + slot * DMA_ALIGN, name=f"raw{chunk}_{c0}")
             nc.sync.dma_start(raw[:], w_rows[:, chunk, :, c0:c1])
             raws[chunk, c0] = raw[:]
 
@@ -78,7 +83,7 @@ def tile_picked_merge_lin_relu_sub_e_kernel(tc, xT, w, b, offs, out):
             )
 
         def new_part(chunk, c0, c1):
-            groupeds[chunk, c0] = held.tile([P, c1 - c0, PACK], BF16, align_bytes=64, name=f"w_grouped{chunk}_{c0}")
+            groupeds[chunk, c0] = held.tile([P, c1 - c0, PACK], BF16, align_bytes=LINE_ALIGN, name=f"w_grouped{chunk}_{c0}")
 
         def spread(chunk, load0, part0, c0, c1, engine_copy):
             interleave(
@@ -88,8 +93,8 @@ def tile_picked_merge_lin_relu_sub_e_kernel(tc, xT, w, b, offs, out):
             )
 
         def finish_part(chunk, c0, c1):
-            w_codes = held.tile([P, c1 - c0], U32, align_bytes=64, name=f"w_codes{chunk}_{c0}")
-            w_scales = held.tile([P, c1 - c0], U8, align_bytes=64, name=f"w_scales{chunk}_{c0}")
+            w_codes = held.tile([P, c1 - c0], U32, align_bytes=LINE_ALIGN, name=f"w_codes{chunk}_{c0}")
+            w_scales = held.tile([P, c1 - c0], U8, align_bytes=LINE_ALIGN, name=f"w_scales{chunk}_{c0}")
             nc.vector.quantize_mx(
                 out=w_codes[:].bitcast(FP8X4),
                 scales=w_scales[:],
@@ -132,9 +137,9 @@ def tile_picked_merge_lin_relu_sub_e_kernel(tc, xT, w, b, offs, out):
         load_chunks(5, 1)
         load_chunks(6, 1)
         last = D * PASSES - 1
-        load_columns(last, 0, 256)
-        load_columns(last, 256, 384)
-        load_columns(last, 384, 512)
+        load_columns(last, 0, 256, 0)
+        load_columns(last, 256, 384, 1)
+        load_columns(last, 384, 512, 2)
 
         gather(0)
         interleave(x_grouped[0][:], picked[0][:], nc.scalar.copy)
@@ -145,7 +150,7 @@ def tile_picked_merge_lin_relu_sub_e_kernel(tc, xT, w, b, offs, out):
         share = 224
         new_part(0, 0, N)
         spread(0, 0, 0, 0, N, nc.scalar.copy)
-        x_grouped[1] = held.tile([P, S, PACK], BF16, align_bytes=DMA_ALIGN, name="x_grouped1", tag="raw0")
+        x_grouped[1] = moved.tile([P, S, PACK], BF16, align_bytes=DMA_ALIGN, offset=W_AT, name="x_grouped1", tag="raw0")
         interleave(x_grouped[1][:, :share, :], picked[1][:, :, :share], nc.vector.tensor_copy)
         interleave(x_grouped[1][:, share:, :], picked[1][:, :, share:], nc.scalar.copy)
         finish_part(0, 0, N)

@@ -20,6 +20,7 @@ PACK = 4
 K_PASS = P * PACK
 PASSES = K // K_PASS
 M_TILES = N // P
+FIRST = 4
 DMA_ALIGN = 4096
 LINE_ALIGN = 256
 PLANES_BYTES = PACK * T * 4
@@ -100,17 +101,30 @@ def tile_picked_merge_lin_relu_sub_e_kernel(tc, xT, w, b, offs, out):
                 scales=w_scales[:],
                 in_=groupeds[chunk, c0][:].rearrange("p c j -> p (c j)"),
             )
+            codes[chunk, c0], scales[chunk, c0] = w_codes, w_scales
+            if chunk >= FIRST:
+                multiply(chunk, c0, c0, c1)
+            if chunk == FIRST:
+                for earlier in range(FIRST - 1):
+                    multiply(earlier, 0, 0, N)
+            if chunk == FIRST + 1:
+                multiply(FIRST - 1, 0, N // 2, N)
+            if chunk == FIRST + 2:
+                multiply(FIRST - 1, 0, 0, N // 2)
+
+        def multiply(chunk, part0, c0, c1):
+            w_codes, w_scales = codes[chunk, part0], scales[chunk, part0]
             d, a = divmod(chunk, PASSES)
             tokens = slice(d * V, (d + 1) * V)
             for m0 in range(c0, c1, P):
-                cols = slice(m0 - c0, m0 - c0 + P)
+                cols = slice(m0 - part0, m0 - part0 + P)
                 nc.tensor.matmul_mx(
                     out=acc[m0 // P][:],
                     lhsT=w_codes[:, cols].bitcast(FP8X4),
                     lhsT_scale=w_scales[:, cols],
                     rhs=x_codes[a][:, tokens].bitcast(FP8X4),
                     rhs_scale=x_scales[a][:, tokens],
-                    start=chunk == 0,
+                    start=chunk == FIRST,
                     stop=chunk == D * PASSES - 1,
                 )
 

@@ -20,7 +20,7 @@ PACK = 4
 K_PASS = P * PACK
 PASSES = K // K_PASS
 M_TILES = N // P
-FIRST = 4
+FIRST = 3
 DMA_ALIGN = 4096
 LINE_ALIGN = 256
 PLANES_BYTES = PACK * T * 4
@@ -104,13 +104,14 @@ def tile_picked_merge_lin_relu_sub_e_kernel(tc, xT, w, b, offs, out):
             codes[chunk, c0], scales[chunk, c0] = w_codes, w_scales
             if chunk >= FIRST:
                 multiply(chunk, c0, c0, c1)
-            if chunk == FIRST:
-                for earlier in range(FIRST - 1):
-                    multiply(earlier, 0, 0, N)
-            if chunk == FIRST + 1:
-                multiply(FIRST - 1, 0, N // 2, N)
-            if chunk == FIRST + 2:
-                multiply(FIRST - 1, 0, 0, N // 2)
+            if chunk == 3:
+                multiply(0, 0, 0, N)
+            if chunk == 4:
+                multiply(1, 0, N // 2, N)
+            if chunk == 5:
+                multiply(2, 0, 0, N)
+            if chunk == 6 and c0 == 0:
+                multiply(1, 0, 0, N // 2)
 
         def multiply(chunk, part0, c0, c1):
             w_codes, w_scales = codes[chunk, part0], scales[chunk, part0]
@@ -145,9 +146,9 @@ def tile_picked_merge_lin_relu_sub_e_kernel(tc, xT, w, b, offs, out):
         nc.sync.dma_start(offsets[:], offs)
         nc.sync.dma_start(bias_rows[0:M_TILES, :], b.rearrange("(t p) o -> t (p o)", p=P))
         nc.sync.dma_start(planes[1][:], x_rows[1])
-        load_chunks(0, 1)
-        load_chunks(1, 2)
-        load_chunks(3, 2)
+        load_chunks(0, 2)
+        load_chunks(2, 2)
+        load_chunks(4, 1)
         load_chunks(5, 1)
         load_chunks(6, 1)
         last = D * PASSES - 1
@@ -164,32 +165,31 @@ def tile_picked_merge_lin_relu_sub_e_kernel(tc, xT, w, b, offs, out):
         share = 224
         new_part(0, 0, N)
         spread(0, 0, 0, 0, N, nc.scalar.copy)
-        x_grouped[1] = moved.tile([P, S, PACK], BF16, align_bytes=DMA_ALIGN, offset=W_AT, name="x_grouped1", tag="raw0")
-        interleave(x_grouped[1][:, :share, :], picked[1][:, :, :share], nc.vector.tensor_copy)
-        interleave(x_grouped[1][:, share:, :], picked[1][:, :, share:], nc.scalar.copy)
-        finish_part(0, 0, N)
+        x_grouped[1] = held.tile([P, S, PACK], BF16, align_bytes=LINE_ALIGN, name="x_grouped1")
+        interleave(x_grouped[1][:], picked[1][:], nc.vector.tensor_copy)
+        quantise_x(1)
         for chunk in range(1, last - 1):
             new_part(chunk, 0, N)
-            spread(chunk, 0, 0, 0, share, nc.vector.tensor_copy)
-            spread(chunk, 0, 0, share, N, nc.scalar.copy)
-            if chunk == 1:
-                quantise_x(1)
-            else:
-                finish_part(chunk - 1, 0, N)
+            cut = 320 if chunk == last - 2 else share
+            spread(chunk, 0, 0, 0, cut, nc.vector.tensor_copy)
+            spread(chunk, 0, 0, cut, N, nc.scalar.copy)
+            finish_part(chunk - 1, 0, N)
         finish_part(last - 2, 0, N)
-        new_part(last - 1, 0, N)
+        new_part(last - 1, 0, 256)
+        new_part(last - 1, 256, N)
         spread(last - 1, 0, 0, 0, 256, nc.vector.tensor_copy)
-        spread(last - 1, 0, 0, 256, N, nc.scalar.copy)
+        spread(last - 1, 0, 256, 256, N, nc.scalar.copy)
+        finish_part(last - 1, 0, 256)
         new_part(last, 0, 256)
         new_part(last, 256, 384)
         new_part(last, 384, 512)
-        spread(last, 0, 0, 0, 128, nc.vector.tensor_copy)
-        spread(last, 0, 0, 128, 256, nc.scalar.copy)
-        finish_part(last - 1, 0, N)
+        spread(last, 0, 0, 0, 144, nc.vector.tensor_copy)
+        spread(last, 0, 0, 144, 256, nc.scalar.copy)
+        finish_part(last - 1, 256, N)
         spread(last, 256, 256, 256, 384, nc.scalar.copy)
         finish_part(last, 0, 256)
-        spread(last, 384, 384, 384, 448, nc.vector.tensor_copy)
-        spread(last, 384, 384, 448, 512, nc.scalar.copy)
+        spread(last, 384, 384, 384, 456, nc.vector.tensor_copy)
+        spread(last, 384, 384, 456, 512, nc.scalar.copy)
         finish_part(last, 256, 384)
         finish_part(last, 384, 512)
         emit(0)

@@ -40,7 +40,6 @@ def tile_picked_merge_lin_relu_sub_e_kernel(tc, xT, w, b, offs, out):
 
         offsets = held.tile([P, S // 16], U16, align_bytes=LINE_ALIGN, name="offsets")
         bias_rows = held.tile([P, P], F32, align_bytes=LINE_ALIGN, name="bias_rows")
-        bias = held.tile([P, M_TILES], F32, align_bytes=LINE_ALIGN, name="bias")
         ident = held.tile([P, P], F32, align_bytes=LINE_ALIGN, name="ident")
         raws, groupeds, codes, scales = {}, {}, {}, {}
         planes = [moved.tile([P, PACK, T], F32, align_bytes=DMA_ALIGN, offset=a * PLANES_BYTES, name=f"planes{a}") for a in range(PASSES)]
@@ -144,7 +143,7 @@ def tile_picked_merge_lin_relu_sub_e_kernel(tc, xT, w, b, offs, out):
 
         nc.sync.dma_start(planes[0][:], x_rows[0])
         nc.sync.dma_start(offsets[:], offs)
-        nc.sync.dma_start(bias_rows[0:M_TILES, :], b.rearrange("(t p) o -> t (p o)", p=P))
+        nc.scalar.dma_start(bias_rows[0:M_TILES, :], b.rearrange("(t p) o -> t (p o)", p=P))
         nc.sync.dma_start(planes[1][:], x_rows[1])
         load_chunks(0, 2)
         load_chunks(2, 2)
@@ -158,9 +157,10 @@ def tile_picked_merge_lin_relu_sub_e_kernel(tc, xT, w, b, offs, out):
 
         gather(0)
         interleave(x_grouped[0][:], picked[0][:], nc.scalar.copy)
-        nc.tensor.transpose(turned[:], bias_rows[:], ident[:])
-        nc.vector.tensor_copy(bias[:], turned[:, 0:M_TILES])
         quantise_x(0)
+        bias = moved.tile([P, M_TILES], F32, align_bytes=DMA_ALIGN, offset=0, name="bias")
+        nc.tensor.transpose(turned[:], bias_rows[:], ident[:])
+        nc.scalar.copy(bias[:], turned[:, 0:M_TILES])
         gather(1)
         share = 224
         new_part(0, 0, N)

@@ -13,25 +13,31 @@ U16 = mybir.dt.uint16
 U8 = mybir.dt.uint8
 FP8X4 = mybir.dt.float8_e4m3fn_x4
 RELU = mybir.ActivationFunctionType.Relu
+COPY = mybir.ActivationFunctionType.Copy
 ADD, MAX = mybir.AluOpType.add, mybir.AluOpType.max
 
 P = 128
 PACK = 4
 K_PASS = P * PACK
 PASSES = K // K_PASS
+CHUNKS = D * PASSES
 M_TILES = N // P
-FIRST = 3
+HALF = S // 2
+EARLY = 3
+OPENING = 4
 DMA_ALIGN = 4096
 LINE_ALIGN = 256
 PLANES_BYTES = PACK * T * 4
 CHUNK_BYTES = PACK * N * 4
 W_AT = PASSES * PLANES_BYTES
+SHARE = 224
 
 
 def tile_picked_merge_lin_relu_sub_e_kernel(tc, xT, w, b, offs, out):
     nc = tc.nc
     x_rows = xT.rearrange("(a p j) t -> a p j t", a=PASSES, j=PACK)
     w_rows = w.rearrange("d (a p j) m -> p (d a) j m", a=PASSES, j=PACK)
+    out_tiles = out.rearrange("(t p) v -> p t v", p=P)
 
     with ExitStack() as ctx:
         moved = ctx.enter_context(tc.tile_pool(name="moved", bufs=1))
@@ -41,18 +47,14 @@ def tile_picked_merge_lin_relu_sub_e_kernel(tc, xT, w, b, offs, out):
         offsets = held.tile([P, S // 16], U16, align_bytes=LINE_ALIGN, name="offsets")
         bias_rows = held.tile([P, P], F32, align_bytes=LINE_ALIGN, name="bias_rows")
         ident = held.tile([P, P], F32, align_bytes=LINE_ALIGN, name="ident")
-        raws, groupeds, codes, scales = {}, {}, {}, {}
         planes = [moved.tile([P, PACK, T], F32, align_bytes=DMA_ALIGN, offset=a * PLANES_BYTES, name=f"planes{a}") for a in range(PASSES)]
-        picked = [held.tile([P, PACK, S], F32, align_bytes=LINE_ALIGN, name=f"picked{a}") for a in range(PASSES)]
-        x_grouped = {0: held.tile([P, S, PACK], BF16, align_bytes=LINE_ALIGN, name="x_grouped0")}
-        x_codes = [held.tile([P, S], U32, align_bytes=LINE_ALIGN, name=f"x_codes{a}") for a in range(PASSES)]
-        x_scales = [held.tile([P, S], U8, align_bytes=LINE_ALIGN, name=f"x_scales{a}") for a in range(PASSES)]
         acc = [psum.tile([P, V], F32, name=f"acc{t}") for t in range(M_TILES)]
-        result = moved.tile([P, M_TILES, V], F32, align_bytes=DMA_ALIGN, offset=W_AT + D * PASSES * CHUNK_BYTES + DMA_ALIGN, name="result")
-        out_tiles = out.rearrange("(t p) v -> p t v", p=P)
+        turned = psum.tile([P, P], F32, name="turned")
+        result = moved.tile([P, M_TILES, V], F32, align_bytes=DMA_ALIGN, offset=W_AT + (CHUNKS + 1) * CHUNK_BYTES, name="result")
+        raws, x_grouped, x_mx, w_grouped, w_mx = {}, {}, {}, {}, {}
 
         def load_chunks(first, count):
-            raw = moved.tile([P, count, PACK, N], F32, align_bytes=DMA_ALIGN, offset=W_AT + first * CHUNK_BYTES, name=f"raw{first}", tag=f"raw{first}")
+            raw = moved.tile([P, count, PACK, N], F32, align_bytes=DMA_ALIGN, offset=W_AT + first * CHUNK_BYTES, name=f"raw{first}")
             nc.sync.dma_start(
                 raw[:].rearrange("p c j m -> p c (j m)"),
                 w_rows[:, first : first + count, :, :].rearrange("p c j m -> p c (j m)"),
@@ -71,62 +73,70 @@ def tile_picked_merge_lin_relu_sub_e_kernel(tc, xT, w, b, offs, out):
                 src.rearrange("p j (c i) -> p c j i", i=4),
             )
 
-        def gather(a):
+        def quantise(grouped, width, name):
+            codes = held.tile([P, width], U32, align_bytes=LINE_ALIGN, name=f"{name}_codes")
+            scales = held.tile([P, width], U8, align_bytes=LINE_ALIGN, name=f"{name}_scales")
+            nc.vector.quantize_mx(out=codes[:].bitcast(FP8X4), scales=scales[:], in_=grouped[:].rearrange("p c j -> p (c j)"))
+            return codes, scales
+
+        def scalar_gather(dst, src):
+            nc.scalar.activation(dst, src, COPY)
+
+        def pick(a, h):
+            gather, copy = ((nc.vector.tensor_copy, nc.vector.tensor_copy), (scalar_gather, nc.scalar.copy))[h]
+            picked = held.tile([P, PACK, HALF], F32, align_bytes=LINE_ALIGN, name=f"picked{a}_{h}")
+            entries = offsets[:, h * HALF // 16 : (h + 1) * HALF // 16]
             for j in range(PACK):
-                nc.vector.tensor_copy(picked[a][:, j, :], planes[a][:, j, :].indirect(offsets[:]))
+                gather(picked[:, j, :], planes[a][:, j, :].indirect(entries))
+            x_grouped[a, h] = held.tile([P, HALF, PACK], BF16, align_bytes=LINE_ALIGN, name=f"x_grouped{a}_{h}")
+            interleave(x_grouped[a, h][:], picked[:], copy)
 
         def quantise_x(a):
-            nc.vector.quantize_mx(
-                out=x_codes[a][:].bitcast(FP8X4),
-                scales=x_scales[a][:],
-                in_=x_grouped[a][:].rearrange("p c j -> p (c j)"),
-            )
+            for h in range(2):
+                x_mx[a, h] = quantise(x_grouped[a, h], HALF, f"x{a}_{h}")
 
         def new_part(chunk, c0, c1):
-            groupeds[chunk, c0] = held.tile([P, c1 - c0, PACK], BF16, align_bytes=LINE_ALIGN, name=f"w_grouped{chunk}_{c0}")
+            shape, name = [P, c1 - c0, PACK], f"w_grouped{chunk}_{c0}"
+            if chunk < EARLY:
+                w_grouped[chunk, c0] = held.tile(shape, BF16, align_bytes=LINE_ALIGN, name=name)
+            else:
+                at = PLANES_BYTES + ((chunk - EARLY) * N + c0) * PACK * 2
+                w_grouped[chunk, c0] = moved.tile(shape, BF16, align_bytes=LINE_ALIGN, offset=at, name=name)
 
         def spread(chunk, load0, part0, c0, c1, engine_copy):
             interleave(
-                groupeds[chunk, part0][:, c0 - part0 : c1 - part0, :],
+                w_grouped[chunk, part0][:, c0 - part0 : c1 - part0, :],
                 raws[chunk, load0][:, :, c0 - load0 : c1 - load0],
                 engine_copy,
             )
 
-        def finish_part(chunk, c0, c1):
-            w_codes = held.tile([P, c1 - c0], U32, align_bytes=LINE_ALIGN, name=f"w_codes{chunk}_{c0}")
-            w_scales = held.tile([P, c1 - c0], U8, align_bytes=LINE_ALIGN, name=f"w_scales{chunk}_{c0}")
-            nc.vector.quantize_mx(
-                out=w_codes[:].bitcast(FP8X4),
-                scales=w_scales[:],
-                in_=groupeds[chunk, c0][:].rearrange("p c j -> p (c j)"),
-            )
-            codes[chunk, c0], scales[chunk, c0] = w_codes, w_scales
-            if chunk >= FIRST:
-                multiply(chunk, c0, c0, c1)
-            if chunk == 3:
-                multiply(0, 0, 0, N)
-            if chunk == 4:
-                multiply(1, 0, N // 2, N)
-            if chunk == 5:
-                multiply(2, 0, 0, N)
-            if chunk == 6 and c0 == 0:
-                multiply(1, 0, 0, N // 2)
+        def spread_chunk(chunk, share):
+            new_part(chunk, 0, N)
+            spread(chunk, 0, 0, 0, share, nc.vector.tensor_copy)
+            spread(chunk, 0, 0, share, N, nc.scalar.copy)
 
-        def multiply(chunk, part0, c0, c1):
-            w_codes, w_scales = codes[chunk, part0], scales[chunk, part0]
-            d, a = divmod(chunk, PASSES)
-            tokens = slice(d * V, (d + 1) * V)
+        def quantise_w(chunk, c0, c1):
+            codes, scales = quantise(w_grouped[chunk, c0], c1 - c0, f"w{chunk}_{c0}")
             for m0 in range(c0, c1, P):
-                cols = slice(m0 - part0, m0 - part0 + P)
-                nc.tensor.matmul_mx(
-                    out=acc[m0 // P][:],
-                    lhsT=w_codes[:, cols].bitcast(FP8X4),
-                    lhsT_scale=w_scales[:, cols],
-                    rhs=x_codes[a][:, tokens].bitcast(FP8X4),
-                    rhs_scale=x_scales[a][:, tokens],
-                    start=chunk == FIRST,
-                    stop=chunk == D * PASSES - 1,
-                )
+                cols = slice(m0 - c0, m0 - c0 + P)
+                w_mx[chunk, m0 // P] = (codes[:, cols], scales[:, cols])
+
+        def multiply(chunks, tiles):
+            for chunk in chunks:
+                d, a = divmod(chunk, PASSES)
+                h, place = divmod(d * V, HALF)
+                x_codes, x_scales = x_mx[a, h]
+                for t in tiles:
+                    w_codes, w_scales = w_mx[chunk, t]
+                    nc.tensor.matmul_mx(
+                        out=acc[t][:],
+                        lhsT=w_codes.bitcast(FP8X4),
+                        lhsT_scale=w_scales,
+                        rhs=x_codes[:, place : place + V].bitcast(FP8X4),
+                        rhs_scale=x_scales[:, place : place + V],
+                        start=chunk == OPENING,
+                        stop=chunk == CHUNKS - 1,
+                    )
 
         def emit(t, on_vector=False):
             if on_vector:
@@ -139,59 +149,62 @@ def tile_picked_merge_lin_relu_sub_e_kernel(tc, xT, w, b, offs, out):
 
         nc.gpsimd.memset(bias_rows[:], 0.0)
         make_identity(nc, ident[:])
-        turned = psum.tile([P, P], F32, name="turned")
 
+        last = CHUNKS - 1
         nc.sync.dma_start(planes[0][:], x_rows[0])
         nc.sync.dma_start(offsets[:], offs)
         nc.scalar.dma_start(bias_rows[0:M_TILES, :], b.rearrange("(t p) o -> t (p o)", p=P))
+        load_chunks(0, EARLY)
         nc.sync.dma_start(planes[1][:], x_rows[1])
-        load_chunks(0, 2)
-        load_chunks(2, 2)
-        load_chunks(4, 1)
+        load_chunks(EARLY, 2)
         load_chunks(5, 1)
         load_chunks(6, 1)
-        last = D * PASSES - 1
         load_columns(last, 0, 256, 0)
         load_columns(last, 256, 384, 1)
         load_columns(last, 384, 512, 2)
 
-        gather(0)
-        interleave(x_grouped[0][:], picked[0][:], nc.scalar.copy)
+        pick(0, 0)
+        pick(0, 1)
         quantise_x(0)
         bias = moved.tile([P, M_TILES], F32, align_bytes=DMA_ALIGN, offset=0, name="bias")
         nc.tensor.transpose(turned[:], bias_rows[:], ident[:])
         nc.scalar.copy(bias[:], turned[:, 0:M_TILES])
-        gather(1)
-        share = 224
-        new_part(0, 0, N)
-        spread(0, 0, 0, 0, N, nc.scalar.copy)
-        x_grouped[1] = held.tile([P, S, PACK], BF16, align_bytes=LINE_ALIGN, name="x_grouped1")
-        interleave(x_grouped[1][:], picked[1][:], nc.vector.tensor_copy)
+        for chunk in range(EARLY):
+            spread_chunk(chunk, SHARE)
+            quantise_w(chunk, 0, N)
+        pick(1, 0)
+        pick(1, 1)
         quantise_x(1)
-        for chunk in range(1, last - 1):
-            new_part(chunk, 0, N)
-            cut = 320 if chunk == last - 2 else share
-            spread(chunk, 0, 0, 0, cut, nc.vector.tensor_copy)
-            spread(chunk, 0, 0, cut, N, nc.scalar.copy)
-            finish_part(chunk - 1, 0, N)
-        finish_part(last - 2, 0, N)
+        spread_chunk(3, 288)
+        spread_chunk(4, 288)
+        quantise_w(3, 0, N)
+        quantise_w(4, 0, N)
+        multiply([4], range(M_TILES))
+        spread_chunk(5, 192)
+        quantise_w(5, 0, N)
+        multiply([5, 0, 1], range(M_TILES))
         new_part(last - 1, 0, 256)
         new_part(last - 1, 256, N)
         spread(last - 1, 0, 0, 0, 256, nc.vector.tensor_copy)
         spread(last - 1, 0, 256, 256, N, nc.scalar.copy)
-        finish_part(last - 1, 0, 256)
+        quantise_w(last - 1, 0, 256)
+        multiply([6, 2, 3], [0, 1])
         new_part(last, 0, 256)
         new_part(last, 256, 384)
         new_part(last, 384, 512)
         spread(last, 0, 0, 0, 144, nc.vector.tensor_copy)
         spread(last, 0, 0, 144, 256, nc.scalar.copy)
-        finish_part(last - 1, 256, N)
+        quantise_w(last - 1, 256, N)
+        multiply([6, 2, 3], [2, 3])
         spread(last, 256, 256, 256, 384, nc.scalar.copy)
-        finish_part(last, 0, 256)
+        quantise_w(last, 0, 256)
+        multiply([last], [0, 1])
         spread(last, 384, 384, 384, 456, nc.vector.tensor_copy)
         spread(last, 384, 384, 456, 512, nc.scalar.copy)
-        finish_part(last, 256, 384)
-        finish_part(last, 384, 512)
+        quantise_w(last, 256, 384)
+        multiply([last], [2])
+        quantise_w(last, 384, 512)
+        multiply([last], [3])
         emit(0)
         emit(1)
         store(0, 2, nc.scalar)

@@ -22,7 +22,6 @@ K_PASS = P * PACK
 PASSES = K // K_PASS
 CHUNKS = D * PASSES
 M_TILES = N // P
-HALF = S // 2
 EARLY = 3
 OPENING = 4
 DMA_ALIGN = 4096
@@ -30,7 +29,6 @@ LINE_ALIGN = 256
 PLANES_BYTES = PACK * T * 4
 CHUNK_BYTES = PACK * N * 4
 W_AT = PASSES * PLANES_BYTES
-SHARE = 224
 
 
 def tile_picked_merge_lin_relu_sub_e_kernel(tc, xT, w, b, offs, out):
@@ -51,7 +49,7 @@ def tile_picked_merge_lin_relu_sub_e_kernel(tc, xT, w, b, offs, out):
         acc = [psum.tile([P, V], F32, name=f"acc{t}") for t in range(M_TILES)]
         turned = psum.tile([P, P], F32, name="turned")
         result = moved.tile([P, M_TILES, V], F32, align_bytes=DMA_ALIGN, offset=W_AT + (CHUNKS + 1) * CHUNK_BYTES, name="result")
-        raws, x_grouped, x_mx, w_grouped, w_mx = {}, {}, {}, {}, {}
+        raws, x_mx, w_grouped, w_mx = {}, {}, {}, {}
 
         def load_chunks(first, count):
             raw = moved.tile([P, count, PACK, N], F32, align_bytes=DMA_ALIGN, offset=W_AT + first * CHUNK_BYTES, name=f"raw{first}")
@@ -82,26 +80,17 @@ def tile_picked_merge_lin_relu_sub_e_kernel(tc, xT, w, b, offs, out):
         def scalar_gather(dst, src):
             nc.scalar.activation(dst, src, COPY)
 
-        def pick(a, h):
-            gather, copy = ((nc.vector.tensor_copy, nc.vector.tensor_copy), (scalar_gather, nc.scalar.copy))[h]
-            picked = held.tile([P, PACK, HALF], F32, align_bytes=LINE_ALIGN, name=f"picked{a}_{h}")
-            entries = offsets[:, h * HALF // 16 : (h + 1) * HALF // 16]
+        def prepare_x(a, engine_copy):
+            picked = held.tile([P, PACK, S], F32, align_bytes=LINE_ALIGN, name=f"picked{a}")
             for j in range(PACK):
-                gather(picked[:, j, :], planes[a][:, j, :].indirect(entries))
-            x_grouped[a, h] = held.tile([P, HALF, PACK], BF16, align_bytes=LINE_ALIGN, name=f"x_grouped{a}_{h}")
-            interleave(x_grouped[a, h][:], picked[:], copy)
-
-        def quantise_x(a):
-            for h in range(2):
-                x_mx[a, h] = quantise(x_grouped[a, h], HALF, f"x{a}_{h}")
+                gather = nc.vector.tensor_copy if j < PACK // 2 else scalar_gather
+                gather(picked[:, j, :], planes[a][:, j, :].indirect(offsets[:]))
+            grouped = held.tile([P, S, PACK], BF16, align_bytes=LINE_ALIGN, name=f"x_grouped{a}")
+            interleave(grouped[:], picked[:], engine_copy)
+            x_mx[a] = quantise(grouped, S, f"x{a}")
 
         def new_part(chunk, c0, c1):
-            shape, name = [P, c1 - c0, PACK], f"w_grouped{chunk}_{c0}"
-            if chunk < EARLY:
-                w_grouped[chunk, c0] = held.tile(shape, BF16, align_bytes=LINE_ALIGN, name=name)
-            else:
-                at = PLANES_BYTES + ((chunk - EARLY) * N + c0) * PACK * 2
-                w_grouped[chunk, c0] = moved.tile(shape, BF16, align_bytes=LINE_ALIGN, offset=at, name=name)
+            w_grouped[chunk, c0] = held.tile([P, c1 - c0, PACK], BF16, align_bytes=LINE_ALIGN, name=f"w_grouped{chunk}_{c0}")
 
         def spread(chunk, load0, part0, c0, c1, engine_copy):
             interleave(
@@ -112,8 +101,10 @@ def tile_picked_merge_lin_relu_sub_e_kernel(tc, xT, w, b, offs, out):
 
         def spread_chunk(chunk, share):
             new_part(chunk, 0, N)
-            spread(chunk, 0, 0, 0, share, nc.vector.tensor_copy)
-            spread(chunk, 0, 0, share, N, nc.scalar.copy)
+            if share > 0:
+                spread(chunk, 0, 0, 0, share, nc.vector.tensor_copy)
+            if share < N:
+                spread(chunk, 0, 0, share, N, nc.scalar.copy)
 
         def quantise_w(chunk, c0, c1):
             codes, scales = quantise(w_grouped[chunk, c0], c1 - c0, f"w{chunk}_{c0}")
@@ -124,16 +115,16 @@ def tile_picked_merge_lin_relu_sub_e_kernel(tc, xT, w, b, offs, out):
         def multiply(chunks, tiles):
             for chunk in chunks:
                 d, a = divmod(chunk, PASSES)
-                h, place = divmod(d * V, HALF)
-                x_codes, x_scales = x_mx[a, h]
+                x_codes, x_scales = x_mx[a]
+                tokens = slice(d * V, (d + 1) * V)
                 for t in tiles:
                     w_codes, w_scales = w_mx[chunk, t]
                     nc.tensor.matmul_mx(
                         out=acc[t][:],
                         lhsT=w_codes.bitcast(FP8X4),
                         lhsT_scale=w_scales,
-                        rhs=x_codes[:, place : place + V].bitcast(FP8X4),
-                        rhs_scale=x_scales[:, place : place + V],
+                        rhs=x_codes[:, tokens].bitcast(FP8X4),
+                        rhs_scale=x_scales[:, tokens],
                         start=chunk == OPENING,
                         stop=chunk == CHUNKS - 1,
                     )
@@ -154,8 +145,8 @@ def tile_picked_merge_lin_relu_sub_e_kernel(tc, xT, w, b, offs, out):
         nc.sync.dma_start(planes[0][:], x_rows[0])
         nc.sync.dma_start(offsets[:], offs)
         nc.scalar.dma_start(bias_rows[0:M_TILES, :], b.rearrange("(t p) o -> t (p o)", p=P))
-        load_chunks(0, EARLY)
         nc.sync.dma_start(planes[1][:], x_rows[1])
+        load_chunks(0, EARLY)
         load_chunks(EARLY, 2)
         load_chunks(5, 1)
         load_chunks(6, 1)
@@ -163,26 +154,24 @@ def tile_picked_merge_lin_relu_sub_e_kernel(tc, xT, w, b, offs, out):
         load_columns(last, 256, 384, 1)
         load_columns(last, 384, 512, 2)
 
-        pick(0, 0)
-        pick(0, 1)
-        quantise_x(0)
+        prepare_x(0, nc.scalar.copy)
         bias = moved.tile([P, M_TILES], F32, align_bytes=DMA_ALIGN, offset=0, name="bias")
         nc.tensor.transpose(turned[:], bias_rows[:], ident[:])
         nc.scalar.copy(bias[:], turned[:, 0:M_TILES])
-        for chunk in range(EARLY):
-            spread_chunk(chunk, SHARE)
+        prepare_x(1, nc.vector.tensor_copy)
+        spread_chunk(0, 0)
+        spread_chunk(1, N)
+        spread_chunk(2, 320)
+        for chunk in (1, 0, 2):
             quantise_w(chunk, 0, N)
-        pick(1, 0)
-        pick(1, 1)
-        quantise_x(1)
-        spread_chunk(3, 288)
-        spread_chunk(4, 288)
+        spread_chunk(3, N)
+        spread_chunk(4, P)
         quantise_w(3, 0, N)
         quantise_w(4, 0, N)
-        multiply([4], range(M_TILES))
-        spread_chunk(5, 192)
+        multiply([4, 0], range(M_TILES))
+        spread_chunk(5, N // 2)
         quantise_w(5, 0, N)
-        multiply([5, 0, 1], range(M_TILES))
+        multiply([5, 1], range(M_TILES))
         new_part(last - 1, 0, 256)
         new_part(last - 1, 256, N)
         spread(last - 1, 0, 0, 0, 256, nc.vector.tensor_copy)
@@ -207,8 +196,8 @@ def tile_picked_merge_lin_relu_sub_e_kernel(tc, xT, w, b, offs, out):
         multiply([last], [3])
         emit(0)
         emit(1)
-        store(0, 2, nc.scalar)
+        store(0, 2, nc.sync)
         emit(2)
-        store(2, 3, nc.scalar)
+        store(2, 3, nc.sync)
         emit(3, on_vector=True)
         store(3, 4, nc.sync)

@@ -22,7 +22,6 @@ K_PASS = P * PACK
 PASSES = K // K_PASS
 CHUNKS = D * PASSES
 M_TILES = N // P
-EARLY = 3
 OPENING = 4
 DMA_ALIGN = 4096
 LINE_ALIGN = 256
@@ -146,8 +145,9 @@ def tile_picked_merge_lin_relu_sub_e_kernel(tc, xT, w, b, offs, out):
         nc.sync.dma_start(offsets[:], offs)
         nc.scalar.dma_start(bias_rows[0:M_TILES, :], b.rearrange("(t p) o -> t (p o)", p=P))
         nc.sync.dma_start(planes[1][:], x_rows[1])
-        load_chunks(0, EARLY)
-        load_chunks(EARLY, 2)
+        load_chunks(0, 2)
+        load_chunks(2, 2)
+        load_chunks(4, 1)
         load_chunks(5, 1)
         load_chunks(6, 1)
         load_columns(last, 0, 256, 0)
@@ -159,17 +159,15 @@ def tile_picked_merge_lin_relu_sub_e_kernel(tc, xT, w, b, offs, out):
         nc.tensor.transpose(turned[:], bias_rows[:], ident[:])
         nc.scalar.copy(bias[:], turned[:, 0:M_TILES])
         prepare_x(1, nc.vector.tensor_copy)
-        spread_chunk(0, 0)
-        spread_chunk(1, N)
-        spread_chunk(2, 320)
-        for chunk in (1, 0, 2):
+        for chunk in (0, 2):
+            spread_chunk(chunk, N)
+            spread_chunk(chunk + 1, P)
             quantise_w(chunk, 0, N)
-        spread_chunk(3, N)
-        spread_chunk(4, P)
-        quantise_w(3, 0, N)
+            quantise_w(chunk + 1, 0, N)
+        spread_chunk(4, 320)
         quantise_w(4, 0, N)
         multiply([4, 0], range(M_TILES))
-        spread_chunk(5, N // 2)
+        spread_chunk(5, 320)
         quantise_w(5, 0, N)
         multiply([5, 1], range(M_TILES))
         new_part(last - 1, 0, 256)

@@ -178,7 +178,8 @@ def tile_picked_merge_lin_relu_sub_e_kernel(tc, xT, w, b, offs, out):
         multiply([6, 2, 3], [0, 1])
         new_part(last, 0, 256)
         new_part(last, 256, 384)
-        new_part(last, 384, 512)
+        new_part(last, 384, 448)
+        new_part(last, 448, 512)
         spread(last, 0, 0, 0, 144, nc.vector.tensor_copy)
         spread(last, 0, 0, 144, 256, nc.scalar.copy)
         quantise_w(last - 1, 256, N)
@@ -186,11 +187,20 @@ def tile_picked_merge_lin_relu_sub_e_kernel(tc, xT, w, b, offs, out):
         spread(last, 256, 256, 256, 384, nc.scalar.copy)
         quantise_w(last, 0, 256)
         multiply([last], [0, 1])
-        spread(last, 384, 384, 384, 456, nc.vector.tensor_copy)
-        spread(last, 384, 384, 456, 512, nc.scalar.copy)
+        spread(last, 384, 384, 384, 448, nc.vector.tensor_copy)
+        spread(last, 384, 448, 448, 512, nc.scalar.copy)
         quantise_w(last, 256, 384)
         multiply([last], [2])
-        quantise_w(last, 384, 512)
+        end_codes = held.tile([P, P], U32, align_bytes=LINE_ALIGN, name="end_codes")
+        end_scales = held.tile([P, P], U8, align_bytes=LINE_ALIGN, name="end_scales")
+        for c0 in (448, 384):
+            cols = slice(c0 - 384, c0 - 384 + 64)
+            nc.vector.quantize_mx(
+                out=end_codes[:, cols].bitcast(FP8X4),
+                scales=end_scales[:, cols],
+                in_=w_grouped[last, c0][:].rearrange("p c j -> p (c j)"),
+            )
+        w_mx[last, 3] = (end_codes[:], end_scales[:])
         multiply([last], [3])
         emit(0)
         emit(1)

@@ -184,9 +184,10 @@ def tile_picked_merge_lin_relu_sub_e_kernel(tc, xT, w, b, offs, out):
         spread(last, 0, 0, 144, 256, nc.scalar.copy)
         quantise_w(last - 1, 256, N)
         multiply([6, 2, 3], [2, 3])
-        spread(last, 256, 256, 256, 384, nc.scalar.copy)
+        spread(last, 256, 256, 288, 384, nc.scalar.copy)
         quantise_w(last, 0, 256)
         multiply([last], [0, 1])
+        spread(last, 256, 256, 256, 288, nc.vector.tensor_copy)
         spread(last, 384, 384, 384, 448, nc.vector.tensor_copy)
         spread(last, 384, 448, 448, 512, nc.scalar.copy)
         quantise_w(last, 256, 384)

@@ -43,6 +43,7 @@ def tile_picked_merge_lin_relu_sub_e_kernel(tc, xT, w, b, offs, out):
 
         offsets = held.tile([P, S // 16], U16, align_bytes=LINE_ALIGN, name="offsets")
         bias_rows = held.tile([P, P], F32, align_bytes=LINE_ALIGN, name="bias_rows")
+        bias_loaded = held.tile([M_TILES, P], F32, align_bytes=LINE_ALIGN, name="bias_loaded")
         ident = held.tile([P, P], F32, align_bytes=LINE_ALIGN, name="ident")
         planes = [moved.tile([P, PACK, T], F32, align_bytes=DMA_ALIGN, offset=a * PLANES_BYTES, name=f"planes{a}") for a in range(PASSES)]
         acc = [psum.tile([P, V], F32, name=f"acc{t}") for t in range(M_TILES)]
@@ -143,7 +144,7 @@ def tile_picked_merge_lin_relu_sub_e_kernel(tc, xT, w, b, offs, out):
         last = CHUNKS - 1
         nc.sync.dma_start(planes[0][:], x_rows[0])
         nc.sync.dma_start(offsets[:], offs)
-        nc.scalar.dma_start(bias_rows[0:M_TILES, :], b.rearrange("(t p) o -> t (p o)", p=P))
+        nc.scalar.dma_start(bias_loaded[:], b.rearrange("(t p) o -> t (p o)", p=P))
         nc.sync.dma_start(planes[1][:], x_rows[1])
         load_chunks(0, 2)
         load_chunks(2, 2)
@@ -154,6 +155,7 @@ def tile_picked_merge_lin_relu_sub_e_kernel(tc, xT, w, b, offs, out):
         load_columns(last, 256, 384, 1)
         load_columns(last, 384, 512, 2)
 
+        nc.gpsimd.tensor_copy(bias_rows[0:M_TILES, :], bias_loaded[:])
         prepare_x(0, nc.scalar.copy)
         bias = moved.tile([P, M_TILES], F32, align_bytes=DMA_ALIGN, offset=0, name="bias")
         nc.tensor.transpose(turned[:], bias_rows[:], ident[:])

@@ -169,15 +169,17 @@ def tile_picked_merge_lin_relu_sub_e_kernel(tc, xT, w, b, offs, out):
         spread_chunk(4, 320)
         quantise_w(4, 0, N)
         multiply([4, 0], range(M_TILES))
+        multiply([1], [0, 1])
         spread_chunk(5, 320)
         quantise_w(5, 0, N)
-        multiply([5, 1], range(M_TILES))
+        multiply([5, 2], range(M_TILES))
+        multiply([1], [2, 3])
         new_part(last - 1, 0, 256)
         new_part(last - 1, 256, N)
         spread(last - 1, 0, 0, 0, 256, nc.vector.tensor_copy)
         spread(last - 1, 0, 256, 256, N, nc.scalar.copy)
         quantise_w(last - 1, 0, 256)
-        multiply([6, 2, 3], [0, 1])
+        multiply([6, 3], [0, 1])
         new_part(last, 0, 256)
         new_part(last, 256, 384)
         new_part(last, 384, 448)
@@ -185,7 +187,7 @@ def tile_picked_merge_lin_relu_sub_e_kernel(tc, xT, w, b, offs, out):
         spread(last, 0, 0, 0, 144, nc.vector.tensor_copy)
         spread(last, 0, 0, 144, 256, nc.scalar.copy)
         quantise_w(last - 1, 256, N)
-        multiply([6, 2, 3], [2, 3])
+        multiply([6, 3], [2, 3])
         spread(last, 256, 256, 288, 384, nc.scalar.copy)
         quantise_w(last, 0, 256)
         multiply([last], [0, 1])

from contextlib import ExitStack

import concourse.mybir as mybir
from concourse.masks import make_identity

K, T, D, S, V, N = 1024, 2048, 4, 512, 128, 512
FLOPS = 2 * K * N * S

F32 = mybir.dt.float32
BF16 = mybir.dt.bfloat16
U32 = mybir.dt.uint32
U16 = mybir.dt.uint16
U8 = mybir.dt.uint8
FP8X4 = mybir.dt.float8_e4m3fn_x4
RELU = mybir.ActivationFunctionType.Relu
COPY = mybir.ActivationFunctionType.Copy
ADD, MAX = mybir.AluOpType.add, mybir.AluOpType.max

P = 128
PACK = 4
K_PASS = P * PACK
PASSES = K // K_PASS
CHUNKS = D * PASSES
M_TILES = N // P
OPENING = 4
DMA_ALIGN = 4096
LINE_ALIGN = 256
PLANES_BYTES = PACK * T * 4
CHUNK_BYTES = PACK * N * 4
W_AT = PASSES * PLANES_BYTES


def tile_picked_merge_lin_relu_sub_e_kernel(tc, xT, w, b, offs, out):
    nc = tc.nc
    x_rows = xT.rearrange("(a p j) t -> a p j t", a=PASSES, j=PACK)
    w_rows = w.rearrange("d (a p j) m -> p (d a) j m", a=PASSES, j=PACK)
    out_tiles = out.rearrange("(t p) v -> p t v", p=P)

    with ExitStack() as ctx:
        moved = ctx.enter_context(tc.tile_pool(name="moved", bufs=1))
        held = ctx.enter_context(tc.tile_pool(name="held", bufs=1))
        psum = ctx.enter_context(tc.psum_pool(name="psum", bufs=1))

        offsets = held.tile([P, S // 16], U16, align_bytes=LINE_ALIGN, name="offsets")
        bias_rows = held.tile([P, P], F32, align_bytes=LINE_ALIGN, name="bias_rows")
        bias_loaded = held.tile([M_TILES, P], F32, align_bytes=LINE_ALIGN, name="bias_loaded")
        ident = held.tile([P, P], F32, align_bytes=LINE_ALIGN, name="ident")
        planes = [moved.tile([P, PACK, T], F32, align_bytes=DMA_ALIGN, offset=a * PLANES_BYTES, name=f"planes{a}") for a in range(PASSES)]
        acc = [psum.tile([P, V], F32, name=f"acc{t}") for t in range(M_TILES)]
        turned = psum.tile([P, P], F32, name="turned")
        result = moved.tile([P, M_TILES, V], F32, align_bytes=DMA_ALIGN, offset=W_AT + (CHUNKS + 1) * CHUNK_BYTES, name="result")
        raws, x_mx, w_grouped, w_mx = {}, {}, {}, {}

        def load_chunks(first, count):
            raw = moved.tile([P, count, PACK, N], F32, align_bytes=DMA_ALIGN, offset=W_AT + first * CHUNK_BYTES, name=f"raw{first}")
            nc.sync.dma_start(
                raw[:].rearrange("p c j m -> p c (j m)"),
                w_rows[:, first : first + count, :, :].rearrange("p c j m -> p c (j m)"),
            )
            for c in range(count):
                raws[first + c, 0] = raw[:, c, :, :]

        def load_columns(chunk, c0, c1, slot):
            raw = moved.tile([P, PACK, c1 - c0], F32, align_bytes=DMA_ALIGN, offset=W_AT + chunk * CHUNK_BYTES + slot * DMA_ALIGN, name=f"raw{chunk}_{c0}")
            nc.sync.dma_start(raw[:], w_rows[:, chunk, :, c0:c1])
            raws[chunk, c0] = raw[:]

        def interleave(dst, src, engine_copy):
            engine_copy(
                dst.rearrange("p (c i) j -> p c j i", i=4),
                src.rearrange("p j (c i) -> p c j i", i=4),
            )

        def quantise(grouped, width, name):
            codes = held.tile([P, width], U32, align_bytes=LINE_ALIGN, name=f"{name}_codes")
            scales = held.tile([P, width], U8, align_bytes=LINE_ALIGN, name=f"{name}_scales")
            nc.vector.quantize_mx(out=codes[:].bitcast(FP8X4), scales=scales[:], in_=grouped[:].rearrange("p c j -> p (c j)"))
            return codes, scales

        def scalar_gather(dst, src):
            nc.scalar.activation(dst, src, COPY)

        def prepare_x(a, engine_copy):
            picked = held.tile([P, PACK, S], F32, align_bytes=LINE_ALIGN, name=f"picked{a}")
            for j in range(PACK):
                gather = nc.vector.tensor_copy if j < PACK // 2 else scalar_gather
                gather(picked[:, j, :], planes[a][:, j, :].indirect(offsets[:]))
            grouped = held.tile([P, S, PACK], BF16, align_bytes=LINE_ALIGN, name=f"x_grouped{a}")
            interleave(grouped[:], picked[:], engine_copy)
            x_mx[a] = quantise(grouped, S, f"x{a}")

        def new_part(chunk, c0, c1):
            w_grouped[chunk, c0] = held.tile([P, c1 - c0, PACK], BF16, align_bytes=LINE_ALIGN, name=f"w_grouped{chunk}_{c0}")

        def spread(chunk, load0, part0, c0, c1, engine_copy):
            interleave(
                w_grouped[chunk, part0][:, c0 - part0 : c1 - part0, :],
                raws[chunk, load0][:, :, c0 - load0 : c1 - load0],
                engine_copy,
            )

        def spread_chunk(chunk, share):
            new_part(chunk, 0, N)
            if share > 0:
                spread(chunk, 0, 0, 0, share, nc.vector.tensor_copy)
            if share < N:
                spread(chunk, 0, 0, share, N, nc.scalar.copy)

        def quantise_w(chunk, c0, c1):
            codes, scales = quantise(w_grouped[chunk, c0], c1 - c0, f"w{chunk}_{c0}")
            for m0 in range(c0, c1, P):
                cols = slice(m0 - c0, m0 - c0 + P)
                w_mx[chunk, m0 // P] = (codes[:, cols], scales[:, cols])

        def multiply(chunks, tiles):
            for chunk in chunks:
                d, a = divmod(chunk, PASSES)
                x_codes, x_scales = x_mx[a]
                tokens = slice(d * V, (d + 1) * V)
                for t in tiles:
                    w_codes, w_scales = w_mx[chunk, t]
                    nc.tensor.matmul_mx(
                        out=acc[t][:],
                        lhsT=w_codes.bitcast(FP8X4),
                        lhsT_scale=w_scales,
                        rhs=x_codes[:, tokens].bitcast(FP8X4),
                        rhs_scale=x_scales[:, tokens],
                        start=chunk == OPENING,
                        stop=chunk == CHUNKS - 1,
                    )

        def emit(t, on_vector=False):
            if on_vector:
                nc.vector.tensor_scalar(result[:, t, :], acc[t][:], bias[:, t : t + 1], 0.0, op0=ADD, op1=MAX)
            else:
                nc.scalar.activation(result[:, t, :], acc[t][:], RELU, bias=bias[:, t : t + 1])

        def store(t0, t1, queue):
            queue.dma_start(out_tiles[:, t0:t1, :], result[:, t0:t1, :])

        nc.gpsimd.memset(bias_rows[:], 0.0)
        make_identity(nc, ident[:])

        last = CHUNKS - 1
        nc.sync.dma_start(planes[0][:], x_rows[0])
        nc.sync.dma_start(offsets[:], offs)
        nc.scalar.dma_start(bias_loaded[:], b.rearrange("(t p) o -> t (p o)", p=P))
        nc.sync.dma_start(planes[1][:], x_rows[1])
        load_chunks(0, 2)
        load_chunks(2, 2)
        load_chunks(4, 1)
        load_chunks(5, 1)
        load_chunks(6, 1)
        load_columns(last, 0, 256, 0)
        load_columns(last, 256, 384, 1)
        load_columns(last, 384, 512, 2)

        nc.gpsimd.tensor_copy(bias_rows[0:M_TILES, :], bias_loaded[:])
        prepare_x(0, nc.scalar.copy)
        bias = moved.tile([P, M_TILES], F32, align_bytes=DMA_ALIGN, offset=0, name="bias")
        nc.tensor.transpose(turned[:], bias_rows[:], ident[:])
        nc.scalar.copy(bias[:], turned[:, 0:M_TILES])
        prepare_x(1, nc.vector.tensor_copy)
        for chunk in (0, 2):
            spread_chunk(chunk, N)
            spread_chunk(chunk + 1, P)
            quantise_w(chunk, 0, N)
            quantise_w(chunk + 1, 0, N)
        spread_chunk(4, 320)
        quantise_w(4, 0, N)
        multiply([4, 0], range(M_TILES))
        multiply([1], [0, 1])
        spread_chunk(5, 320)
        quantise_w(5, 0, N)
        multiply([5, 2], range(M_TILES))
        multiply([1], [2, 3])
        new_part(last - 1, 0, 256)
        new_part(last - 1, 256, N)
        spread(last - 1, 0, 0, 0, 256, nc.vector.tensor_copy)
        spread(last - 1, 0, 256, 256, N, nc.scalar.copy)
        quantise_w(last - 1, 0, 256)
        multiply([6, 3], [0, 1])
        new_part(last, 0, 256)
        new_part(last, 256, 384)
        new_part(last, 384, 448)
        new_part(last, 448, 512)
        spread(last, 0, 0, 0, 144, nc.vector.tensor_copy)
        spread(last, 0, 0, 144, 256, nc.scalar.copy)
        quantise_w(last - 1, 256, N)
        multiply([6, 3], [2, 3])
        spread(last, 256, 256, 288, 384, nc.scalar.copy)
        quantise_w(last, 0, 256)
        multiply([last], [0, 1])
        spread(last, 256, 256, 256, 288, nc.vector.tensor_copy)
        spread(last, 384, 384, 384, 448, nc.vector.tensor_copy)
        spread(last, 384, 448, 448, 512, nc.scalar.copy)
        quantise_w(last, 256, 384)
        multiply([last], [2])
        end_codes = held.tile([P, P], U32, align_bytes=LINE_ALIGN, name="end_codes")
        end_scales = held.tile([P, P], U8, align_bytes=LINE_ALIGN, name="end_scales")
        for c0 in (448, 384):
            cols = slice(c0 - 384, c0 - 384 + 64)
            nc.vector.quantize_mx(
                out=end_codes[:, cols].bitcast(FP8X4),
                scales=end_scales[:, cols],
                in_=w_grouped[last, c0][:].rearrange("p c j -> p (c j)"),
            )
        w_mx[last, 3] = (end_codes[:], end_scales[:])
        multiply([last], [3])
        emit(0)
        emit(1)
        store(0, 2, nc.sync)
        emit(2)
        store(2, 3, nc.sync)
        emit(3, on_vector=True)
        store(3, 4, nc.sync)
